import numpy as np
import ml_dtypes

BF16 = ml_dtypes.bfloat16


def bf(x):
    return np.asarray(x, np.float32).astype(BF16)


def f32(x):
    return np.asarray(x, np.float32)


def f64(x):
    return np.asarray(x).astype(np.float64)


def striped(idx):
    return np.concatenate([l.reshape(-1, 16).T for l in idx])


def rows(idx, k):
    return np.tile(np.repeat(idx, 16, axis=0), (k // (16 * 8), 1))


def look(tab, idx):
    return np.take_along_axis(f64(tab), rows(idx, len(tab)), axis=1)


K, S, V, N, M = 128, 2048, 512, 512, 256


def setup_inputs():
    return {"tab": f32(np.random.standard_normal((K, S))), "w": bf(np.random.standard_normal((K, M)) / np.sqrt(K)), "b": f32(0.5 * np.random.standard_normal((M, 1))), "offs": striped(np.random.randint(0, S, (8, N)))}


def reference(tab, w, b, offs):
    idx = np.stack([g.T.reshape(-1) for g in np.split(offs, 8)])
    t = look(tab, idx)
    x = np.minimum(np.maximum(t, -1.25), 1.0)
    y = f64(w).T @ x
    return y + f64(b)

@@ -1,0 +1,52 @@
+import concourse.mybir as mybir
+
+F32, BF16, U16 = mybir.dt.float32, mybir.dt.bfloat16, mybir.dt.uint16
+ALU = mybir.AluOpType
+ACT = mybir.ActivationFunctionType
+
+P = 128
+LOW, HIGH = -1.25, 1.0
+
+FLOPS = 2 * 128 * 256 * 512
+
+
+def tile_lookup_deq_clip_bias_kernel(tc, tab, w, b, offs, out):
+    nc = tc.nc
+    n_columns = tab.shape[1]
+    n_codes = offs.shape[1] * 16
+    n_features = w.shape[1]
+    n_blocks = n_features // P
+
+    with (
+        tc.tile_pool(name="held", bufs=1) as held,
+        tc.psum_pool(name="psum", bufs=1) as psum,
+    ):
+        offsets = held.tile([P, n_codes // 16], U16, name="offsets")
+        table = held.tile([P, n_columns], F32, name="table")
+        weights = held.tile([P, n_features], BF16, name="weights")
+        biases = [held.tile([P, 1], F32, name=f"bias{k}") for k in range(n_blocks)]
+        nc.scalar.dma_start(table[:], tab)
+        nc.sync.dma_start(offsets[:], offs)
+        nc.sync.dma_start(weights[:], w)
+        for k in range(n_blocks):
+            nc.gpsimd.dma_start(biases[k][:], b[k * P : (k + 1) * P, :])
+
+        clamped = held.tile([P, n_codes], F32, name="clamped")
+        nc.vector.tensor_scalar(
+            clamped[:], table[:].indirect(offsets[:]), LOW, HIGH, op0=ALU.max, op1=ALU.min
+        )
+        x = held.tile([P, n_codes], BF16, name="x")
+        nc.vector.tensor_copy(x[:], clamped[:])
+
+        for k in range(n_blocks):
+            product = psum.tile([P, n_codes], F32, name=f"product{k}")
+            nc.tensor.matmul(
+                product[:], weights[:, k * P : (k + 1) * P], x[:], start=True, stop=True
+            )
+            result = held.tile([P, n_codes], F32, name=f"result{k}")
+            if k % 2 == 0:
+                nc.vector.tensor_scalar_add(result[:], product[:], biases[k][:])
+                nc.sync.dma_start(out[k * P : (k + 1) * P, :], result[:])
+            else:
+                nc.scalar.activation(result[:], product[:], ACT.Identity, bias=biases[k][:])
+                nc.scalar.dma_start(out[k * P : (k + 1) * P, :], result[:])

@@ -35,18 +35,20 @@ def tile_lookup_deq_clip_bias_kernel(tc, tab, w, b, offs, out):
         nc.vector.tensor_scalar(
             clamped[:], table[:].indirect(offsets[:]), LOW, HIGH, op0=ALU.max, op1=ALU.min
         )
-        x = held.tile([P, n_codes], BF16, name="x")
-        nc.vector.tensor_copy(x[:], clamped[:])
 
-        for k in range(n_blocks):
-            product = psum.tile([P, n_codes], F32, name=f"product{k}")
-            nc.tensor.matmul(
-                product[:], weights[:, k * P : (k + 1) * P], x[:], start=True, stop=True
-            )
-            result = held.tile([P, n_codes], F32, name=f"result{k}")
-            if k % 2 == 0:
-                nc.vector.tensor_scalar_add(result[:], product[:], biases[k][:])
-                nc.sync.dma_start(out[k * P : (k + 1) * P, :], result[:])
-            else:
-                nc.scalar.activation(result[:], product[:], ACT.Identity, bias=biases[k][:])
-                nc.scalar.dma_start(out[k * P : (k + 1) * P, :], result[:])
+        half = n_codes // 2
+        for h in range(2):
+            columns = slice(h * half, (h + 1) * half)
+            x = held.tile([P, half], BF16, name=f"x{h}")
+            nc.vector.tensor_copy(x[:], clamped[:, columns])
+            for k in range(n_blocks):
+                features = slice(k * P, (k + 1) * P)
+                product = psum.tile([P, half], F32, name=f"product{h}_{k}")
+                nc.tensor.matmul(product[:], weights[:, features], x[:], start=True, stop=True)
+                result = held.tile([P, half], F32, name=f"result{h}_{k}")
+                if k % 2 == 0:
+                    nc.vector.tensor_scalar_add(result[:], product[:], biases[k][:])
+                    nc.sync.dma_start(out[features, columns], result[:])
+                else:
+                    nc.scalar.activation(result[:], product[:], ACT.Identity, bias=biases[k][:])
+                    nc.scalar.dma_start(out[features, columns], result[:])

@@ -6,6 +6,7 @@ ACT = mybir.ActivationFunctionType
 
 P = 128
 LOW, HIGH = -1.25, 1.0
+ROW_TILE = 32
 
 FLOPS = 2 * 128 * 256 * 512
 
@@ -24,12 +25,26 @@ def tile_lookup_deq_clip_bias_kernel(tc, tab, w, b, offs, out):
         offsets = held.tile([P, n_codes // 16], U16, name="offsets")
         table = held.tile([P, n_columns], F32, name="table")
         weights = held.tile([P, n_features], BF16, name="weights")
-        biases = [held.tile([P, 1], F32, name=f"bias{k}") for k in range(n_blocks)]
+        bias_row = held.tile([ROW_TILE, n_features], F32, name="bias_row")
+        one = held.tile([ROW_TILE, 1], F32, name="one")
+        bias = held.tile([P, n_blocks], F32, name="bias")
         nc.scalar.dma_start(table[:], tab)
         nc.sync.dma_start(offsets[:], offs)
         nc.sync.dma_start(weights[:], w)
+
+        nc.vector.memset(bias_row[:], 0.0)
+        nc.vector.memset(one[:], 1.0)
+        nc.sync.dma_start(bias_row[0:1, :], b.rearrange("m o -> o m"))
+        turned = psum.tile([P, n_blocks], F32, name="turned")
         for k in range(n_blocks):
-            nc.gpsimd.dma_start(biases[k][:], b[k * P : (k + 1) * P, :])
+            nc.tensor.matmul(
+                turned[:, k : k + 1],
+                bias_row[:, k * P : (k + 1) * P],
+                one[:],
+                start=True,
+                stop=True,
+            )
+        nc.scalar.copy(bias[:], turned[:])
 
         clamped = held.tile([P, n_codes], F32, name="clamped")
         nc.vector.tensor_scalar(
@@ -47,8 +62,8 @@ def tile_lookup_deq_clip_bias_kernel(tc, tab, w, b, offs, out):
                 nc.tensor.matmul(product[:], weights[:, features], x[:], start=True, stop=True)
                 result = held.tile([P, half], F32, name=f"result{h}_{k}")
                 if k % 2 == 0:
-                    nc.vector.tensor_scalar_add(result[:], product[:], biases[k][:])
+                    nc.vector.tensor_scalar_add(result[:], product[:], bias[:, k : k + 1])
                     nc.sync.dma_start(out[features, columns], result[:])
                 else:
-                    nc.scalar.activation(result[:], product[:], ACT.Identity, bias=biases[k][:])
+                    nc.scalar.activation(result[:], product[:], ACT.Identity, bias=bias[:, k : k + 1])
                     nc.scalar.dma_start(out[features, columns], result[:])

import concourse.mybir as mybir

F32, BF16, U16 = mybir.dt.float32, mybir.dt.bfloat16, mybir.dt.uint16
ALU = mybir.AluOpType
ACT = mybir.ActivationFunctionType

P = 128
LOW, HIGH = -1.25, 1.0
ROW_TILE = 32

FLOPS = 2 * 128 * 256 * 512


def tile_lookup_deq_clip_bias_kernel(tc, tab, w, b, offs, out):
    nc = tc.nc
    n_columns = tab.shape[1]
    n_codes = offs.shape[1] * 16
    n_features = w.shape[1]
    n_blocks = n_features // P

    with (
        tc.tile_pool(name="held", bufs=1) as held,
        tc.psum_pool(name="psum", bufs=1) as psum,
    ):
        offsets = held.tile([P, n_codes // 16], U16, name="offsets")
        table = held.tile([P, n_columns], F32, name="table")
        weights = held.tile([P, n_features], BF16, name="weights")
        bias_row = held.tile([ROW_TILE, n_features], F32, name="bias_row")
        one = held.tile([ROW_TILE, 1], F32, name="one")
        bias = held.tile([P, n_blocks], F32, name="bias")
        nc.scalar.dma_start(table[:], tab)
        nc.sync.dma_start(offsets[:], offs)
        nc.sync.dma_start(weights[:], w)

        nc.vector.memset(bias_row[:], 0.0)
        nc.vector.memset(one[:], 1.0)
        nc.sync.dma_start(bias_row[0:1, :], b.rearrange("m o -> o m"))
        turned = psum.tile([P, n_blocks], F32, name="turned")
        for k in range(n_blocks):
            nc.tensor.matmul(
                turned[:, k : k + 1],
                bias_row[:, k * P : (k + 1) * P],
                one[:],
                start=True,
                stop=True,
            )
        nc.scalar.copy(bias[:], turned[:])

        clamped = held.tile([P, n_codes], F32, name="clamped")
        nc.vector.tensor_scalar(
            clamped[:], table[:].indirect(offsets[:]), LOW, HIGH, op0=ALU.max, op1=ALU.min
        )

        half = n_codes // 2
        for h in range(2):
            columns = slice(h * half, (h + 1) * half)
            x = held.tile([P, half], BF16, name=f"x{h}")
            nc.vector.tensor_copy(x[:], clamped[:, columns])
            for k in range(n_blocks):
                features = slice(k * P, (k + 1) * P)
                product = psum.tile([P, half], F32, name=f"product{h}_{k}")
                nc.tensor.matmul(product[:], weights[:, features], x[:], start=True, stop=True)
                result = held.tile([P, half], F32, name=f"result{h}_{k}")
                if k % 2 == 0:
                    nc.vector.tensor_scalar_add(result[:], product[:], bias[:, k : k + 1])
                    nc.sync.dma_start(out[features, columns], result[:])
                else:
                    nc.scalar.activation(result[:], product[:], ACT.Identity, bias=bias[:, k : k + 1])
                    nc.scalar.dma_start(out[features, columns], result[:])
